import numpy as np
import ml_dtypes


def mxq(x, axis, fmt="e4m3"):
    dtype, down = {"e4m3": (ml_dtypes.float8_e4m3fn, 7), "e5m2": (ml_dtypes.float8_e5m2, 14)}[fmt]
    v = np.moveaxis(np.asarray(x, np.float32).astype(ml_dtypes.bfloat16).astype(np.float64), axis, -1)
    blocks = v.reshape(v.shape[:-1] + (-1, 32))
    amax = np.abs(blocks).max(-1, keepdims=True)
    byte = np.maximum(np.where(amax > 0, np.frexp(amax)[1] - 1 + 127, 0) - down, 1)
    scale = np.exp2(byte - 127.0)
    codes = (blocks / scale).astype(np.float32).astype(dtype).astype(np.float64)
    return np.moveaxis((codes * scale).reshape(v.shape), -1, axis)


WIDE = False


def mx_kscale(k):
    if not WIDE:
        return np.ones(k)
    levels = np.array([10, -10, 5, -5, 0])
    if k % 512:
        return np.exp2(np.random.permutation(np.resize(levels, k // 32))).repeat(32)
    a = np.empty((k // 512, 16))
    for p in range(k // 512):
        a[p, :8] = np.random.permutation(np.resize(levels, 8))
        for g in range(8):
            far = levels[np.abs(levels - a[p, g]) >= 10]
            a[p, g + 8] = far[np.random.randint(len(far))]
    return np.exp2(a.ravel()).repeat(32)


def f64(x):
    return np.asarray(x).astype(np.float64)


def striped(idx):
    return np.tile(idx.reshape(-1, 16).T, (8, 1)).astype(np.uint16)


def unstriped(offs):
    return offs[:16].T.reshape(-1).astype(np.int64)


def pack_weight(w):
    k, n = w.shape
    w = f64(np.asarray(w, np.float32).astype(ml_dtypes.bfloat16)).reshape(k // 32, 32, n)
    amax = np.abs(w).max(1)
    byte = np.clip(np.where(amax > 0, np.frexp(amax)[1] - 1 + 127 - 7, 1), 1, 254)
    scaled = (w * np.exp2(127.0 - byte)[:, None, :]).reshape(k, n).astype(np.float32)
    words = np.ascontiguousarray(scaled.reshape(k // 512, 128, 4, n).transpose(0, 1, 3, 2)).astype(ml_dtypes.float8_e4m3fn).view(np.uint8)
    return words, np.ascontiguousarray(byte.astype(np.uint8).reshape(k // 512, 16, n))


def unpack_weight(words, scales):
    g, p, n, _ = words.shape
    vals = np.ascontiguousarray(words).view(ml_dtypes.float8_e4m3fn).astype(np.float64) * np.repeat(np.exp2(scales.astype(np.float64) - 127.0), 8, axis=1)[..., None]
    return vals.transpose(0, 1, 3, 2).reshape(g * 512, n)


def relu(v):
    return np.maximum(v, 0.0)


K, T, S, N, U = 1024, 2048, 512, 128, 1024


def setup_inputs():
    n = np.random.standard_normal
    s = mx_kscale(K)[:, None]
    packed_w1 = pack_weight(n((K, N)) / np.sqrt(K) / s)
    return {
        "xT": (n((K, T)) * s).astype(np.float32),
        "w1_words": packed_w1[0],
        "w1_scales": packed_w1[1],
        "scale": np.random.uniform(0.5, 1.5, (N, U)).astype(np.float32),
        "offs": striped(np.random.permutation(T)[:S]),
        "task": striped(np.random.permutation(U)[(U * np.random.uniform(0, 1, S) ** 4).astype(np.int64)]),
    }


def reference(xT, w1_words, w1_scales, scale, offs, task):
    xq = mxq(f64(xT)[:, unstriped(offs)], 0, "e4m3")
    y = unpack_weight(w1_words, w1_scales).T @ xq
    g = f64(scale)[:, unstriped(task)]
    return relu(y * g)

@@ -1,0 +1,102 @@
+from contextlib import ExitStack
+
+import concourse.mybir as mybir
+
+K, T, S, N, U = 1024, 2048, 512, 128, 1024
+FLOPS = 2 * K * S * N
+
+F32 = mybir.dt.float32
+BF16 = mybir.dt.bfloat16
+I32 = mybir.dt.int32
+U32 = mybir.dt.uint32
+U16 = mybir.dt.uint16
+U8 = mybir.dt.uint8
+FP8X4 = mybir.dt.float8_e4m3fn_x4
+
+P = 128
+PACK = 4
+K_PASS = P * PACK
+PASSES = K // K_PASS
+HALVES = 2
+HALF = S // HALVES
+LIST_ROWS = 16
+
+
+def tile_picked_relu_e_kernel(
+    tc, xT, w1_words, w1_scales, scale, offs, task, out
+):
+    nc = tc.nc
+    with ExitStack() as ctx:
+        keep = ctx.enter_context(tc.tile_pool(name="keep", bufs=1))
+        psum = ctx.enter_context(tc.psum_pool(name="psum", bufs=1))
+
+        task_list = keep.tile([P, S // LIST_ROWS], U16, name="task_list")
+        token_list = keep.tile([P, S // LIST_ROWS], U16, name="token_list")
+        scale_table = keep.tile([P, U], F32, name="scale_table")
+        w_codes = keep.tile([P, PASSES, N], U32, name="w_codes", align_bytes=64)
+        w_bytes = keep.tile([P, PASSES, N], U8, name="w_bytes", align_bytes=64)
+
+        nc.sync.dma_start(out=scale_table[:], in_=scale)
+        nc.sync.dma_start(task_list[:], task)
+        nc.sync.dma_start(token_list[:], offs)
+
+        nc.vector.memset(w_bytes[:].rearrange("p z c -> p (z c)").bitcast(I32), 0)
+        for r in range(4):
+            nc.scalar.dma_start(
+                out=w_bytes[r:P:32, :, :].bitcast(I32),
+                in_=w1_scales.rearrange("z (q r) c -> r q z c", r=4)[r].bitcast(I32),
+            )
+
+        x_rows = xT.rearrange("(z p j) t -> z j p t", z=PASSES, j=PACK)
+        planes = {}
+        for z in range(PASSES):
+            for j in range(PACK):
+                planes[z, j] = keep.tile([P, T], F32, name=f"plane_{z}_{j}")
+                nc.sync.dma_start(out=planes[z, j][:], in_=x_rows[z, j])
+        nc.sync.dma_start(
+            out=w_codes[:].bitcast(I32),
+            in_=w1_words.rearrange("z p c r -> p z (c r)").bitcast(I32),
+        )
+
+        gains = keep.tile([P, S], F32, name="gains")
+        nc.vector.tensor_copy(gains[:], scale_table[:].indirect(task_list[:]))
+
+        acc = [psum.tile([P, HALF], F32, name=f"acc_{h}") for h in range(HALVES)]
+        list_cols = HALF // LIST_ROWS
+        for z in range(PASSES):
+            picked = [
+                keep.tile([P, HALF, PACK], BF16, name=f"picked_{z}_{h}", align_bytes=64)
+                for h in range(HALVES)
+            ]
+            for j in range(PACK):
+                for h in range(HALVES):
+                    entries = token_list[:, h * list_cols : (h + 1) * list_cols]
+                    nc.vector.tensor_copy(picked[h][:, :, j], planes[z, j][:].indirect(entries))
+            x_codes, x_bytes = [], []
+            for h in range(HALVES):
+                x_codes.append(keep.tile([P, HALF], U32, name=f"x_codes_{z}_{h}", align_bytes=64))
+                x_bytes.append(keep.tile([P, HALF], U8, name=f"x_bytes_{z}_{h}", align_bytes=64))
+                nc.vector.quantize_mx(
+                    out=x_codes[h][:].bitcast(FP8X4),
+                    scales=x_bytes[h][:],
+                    in_=picked[h][:].rearrange("p s j -> p (s j)"),
+                )
+            for h in range(HALVES):
+                nc.tensor.matmul_mx(
+                    out=acc[h][:],
+                    lhsT=w_codes[:, z, :].bitcast(FP8X4),
+                    lhsT_scale=w_bytes[:, z, :],
+                    rhs=x_codes[h][:].bitcast(FP8X4),
+                    rhs_scale=x_bytes[h][:],
+                    start=(z == 0),
+                    stop=(z == PASSES - 1),
+                )
+
+        for h in range(HALVES):
+            cols = slice(h * HALF, (h + 1) * HALF)
+            scaled = keep.tile([P, HALF], F32, name=f"scaled_{h}")
+            nc.vector.tensor_tensor(scaled[:], acc[h][:], gains[:, cols], mybir.AluOpType.mult)
+            result = keep.tile([P, HALF], F32, name=f"result_{h}")
+            nc.scalar.activation(result[:], scaled[:], mybir.ActivationFunctionType.Relu)
+            queue = nc.scalar if h == HALVES - 1 else nc.sync
+            queue.dma_start(out=out[:, cols], in_=result[:])

@@ -20,6 +20,8 @@ PASSES = K // K_PASS
 HALVES = 2
 HALF = S // HALVES
 LIST_ROWS = 16
+LAST_PLANE = (PASSES - 1, PACK - 1)
+LAST_CHUNKS = ((0, 1024), (1024, 1536), (1536, 2048))
 
 
 def tile_picked_relu_e_kernel(
@@ -36,10 +38,6 @@ def tile_picked_relu_e_kernel(
         w_codes = keep.tile([P, PASSES, N], U32, name="w_codes", align_bytes=64)
         w_bytes = keep.tile([P, PASSES, N], U8, name="w_bytes", align_bytes=64)
 
-        nc.sync.dma_start(out=scale_table[:], in_=scale)
-        nc.sync.dma_start(task_list[:], task)
-        nc.sync.dma_start(token_list[:], offs)
-
         nc.vector.memset(w_bytes[:].rearrange("p z c -> p (z c)").bitcast(I32), 0)
         for r in range(4):
             nc.scalar.dma_start(
@@ -52,51 +50,74 @@ def tile_picked_relu_e_kernel(
         for z in range(PASSES):
             for j in range(PACK):
                 planes[z, j] = keep.tile([P, T], F32, name=f"plane_{z}_{j}")
-                nc.sync.dma_start(out=planes[z, j][:], in_=x_rows[z, j])
+                if (z, j) == LAST_PLANE:
+                    for lo, hi in LAST_CHUNKS:
+                        nc.sync.dma_start(out=planes[z, j][:, lo:hi], in_=x_rows[z, j][:, lo:hi])
+                else:
+                    nc.sync.dma_start(out=planes[z, j][:], in_=x_rows[z, j])
+                if (z, j) == (0, 0):
+                    nc.sync.dma_start(token_list[:], offs)
+                    nc.sync.dma_start(task_list[:], task)
+        nc.sync.dma_start(out=scale_table[:], in_=scale)
         nc.sync.dma_start(
             out=w_codes[:].bitcast(I32),
             in_=w1_words.rearrange("z p c r -> p z (c r)").bitcast(I32),
         )
 
-        gains = keep.tile([P, S], F32, name="gains")
-        nc.vector.tensor_copy(gains[:], scale_table[:].indirect(task_list[:]))
-
-        acc = [psum.tile([P, HALF], F32, name=f"acc_{h}") for h in range(HALVES)]
+        copy = mybir.ActivationFunctionType.Copy
         list_cols = HALF // LIST_ROWS
+        x_codes, x_bytes = {}, {}
         for z in range(PASSES):
             picked = [
                 keep.tile([P, HALF, PACK], BF16, name=f"picked_{z}_{h}", align_bytes=64)
                 for h in range(HALVES)
             ]
             for j in range(PACK):
+                plane = planes[z, j]
+                if (z, j) == LAST_PLANE:
+                    rounded = keep.tile([P, T], BF16, name="rounded", tag="rounded")
+                    for c, (lo, hi) in enumerate(LAST_CHUNKS):
+                        if c % 2 == 0:
+                            nc.scalar.activation(rounded[:, lo:hi], plane[:, lo:hi], copy)
+                        else:
+                            nc.vector.tensor_copy(rounded[:, lo:hi], plane[:, lo:hi])
                 for h in range(HALVES):
                     entries = token_list[:, h * list_cols : (h + 1) * list_cols]
-                    nc.vector.tensor_copy(picked[h][:, :, j], planes[z, j][:].indirect(entries))
-            x_codes, x_bytes = [], []
+                    if (z, j) == LAST_PLANE and h == HALVES - 1:
+                        nc.scalar.activation(picked[h][:, :, j], rounded[:].indirect(entries), copy)
+                    else:
+                        nc.vector.tensor_copy(picked[h][:, :, j], plane[:].indirect(entries))
             for h in range(HALVES):
-                x_codes.append(keep.tile([P, HALF], U32, name=f"x_codes_{z}_{h}", align_bytes=64))
-                x_bytes.append(keep.tile([P, HALF], U8, name=f"x_bytes_{z}_{h}", align_bytes=64))
+                x_codes[z, h] = keep.tile([P, HALF], U32, name=f"x_codes_{z}_{h}", align_bytes=64)
+                x_bytes[z, h] = keep.tile([P, HALF], U8, name=f"x_bytes_{z}_{h}", align_bytes=64)
                 nc.vector.quantize_mx(
-                    out=x_codes[h][:].bitcast(FP8X4),
-                    scales=x_bytes[h][:],
+                    out=x_codes[z, h][:].bitcast(FP8X4),
+                    scales=x_bytes[z, h][:],
                     in_=picked[h][:].rearrange("p s j -> p (s j)"),
                 )
-            for h in range(HALVES):
+
+        reused = keep.tile([P, 2 * HALF], F32, name="reused", tag="rounded")
+        gains_0 = keep.tile([P, HALF], F32, name="gains_0")
+        scaled_1 = keep.tile([P, HALF], F32, name="scaled_1")
+        gains = (gains_0[:], reused[:, :HALF])
+        scaled = (reused[:, HALF:], scaled_1[:])
+        acc = [psum.tile([P, HALF], F32, name=f"acc_{h}") for h in range(HALVES)]
+        for h in range(HALVES):
+            for z in range(PASSES):
                 nc.tensor.matmul_mx(
                     out=acc[h][:],
                     lhsT=w_codes[:, z, :].bitcast(FP8X4),
                     lhsT_scale=w_bytes[:, z, :],
-                    rhs=x_codes[h][:].bitcast(FP8X4),
-                    rhs_scale=x_bytes[h][:],
+                    rhs=x_codes[z, h][:].bitcast(FP8X4),
+                    rhs_scale=x_bytes[z, h][:],
                     start=(z == 0),
                     stop=(z == PASSES - 1),
                 )
-
+            tasks = task_list[:, h * list_cols : (h + 1) * list_cols]
+            nc.vector.tensor_copy(gains[h], scale_table[:].indirect(tasks))
         for h in range(HALVES):
-            cols = slice(h * HALF, (h + 1) * HALF)
-            scaled = keep.tile([P, HALF], F32, name=f"scaled_{h}")
-            nc.vector.tensor_tensor(scaled[:], acc[h][:], gains[:, cols], mybir.AluOpType.mult)
+            nc.vector.tensor_tensor(scaled[h], acc[h][:], gains[h], mybir.AluOpType.mult)
             result = keep.tile([P, HALF], F32, name=f"result_{h}")
-            nc.scalar.activation(result[:], scaled[:], mybir.ActivationFunctionType.Relu)
+            nc.scalar.activation(result[:], scaled[h], mybir.ActivationFunctionType.Relu)
             queue = nc.scalar if h == HALVES - 1 else nc.sync
-            queue.dma_start(out=out[:, cols], in_=result[:])
+            queue.dma_start(out=out[:, h * HALF : (h + 1) * HALF], in_=result[:])

@@ -72,7 +72,14 @@ def tile_picked_relu_e_kernel(
                 keep.tile([P, HALF, PACK], BF16, name=f"picked_{z}_{h}", align_bytes=64)
                 for h in range(HALVES)
             ]
-            for j in range(PACK):
+            if z == PASSES - 1:
+                dense = keep.tile([P, 2, S], BF16, name="dense")
+                for j in range(2):
+                    nc.vector.tensor_copy(dense[:, j, :], planes[z, j][:].indirect(token_list[:]))
+                for h in range(HALVES):
+                    part = dense[:, :, h * HALF : (h + 1) * HALF]
+                    nc.vector.tensor_copy(picked[h][:, :, 0:2], part.rearrange("p j s -> p s j"))
+            for j in range(2 if z == PASSES - 1 else 0, PACK):
                 plane = planes[z, j]
                 if (z, j) == LAST_PLANE:
                     rounded = keep.tile([P, T], BF16, name="rounded", tag="rounded")

@@ -21,7 +21,8 @@ HALVES = 2
 HALF = S // HALVES
 LIST_ROWS = 16
 LAST_PLANE = (PASSES - 1, PACK - 1)
-LAST_CHUNKS = ((0, 1024), (1024, 1536), (1536, 2048))
+LAST_CHUNKS = ((0, 1024), (1024, 1664), (1664, 2048))
+OUT_PIECES = ((0, 0, 256), (1, 0, 128), (1, 128, 256))
 
 
 def tile_picked_relu_e_kernel(
@@ -39,11 +40,6 @@ def tile_picked_relu_e_kernel(
         w_bytes = keep.tile([P, PASSES, N], U8, name="w_bytes", align_bytes=64)
 
         nc.vector.memset(w_bytes[:].rearrange("p z c -> p (z c)").bitcast(I32), 0)
-        for r in range(4):
-            nc.scalar.dma_start(
-                out=w_bytes[r:P:32, :, :].bitcast(I32),
-                in_=w1_scales.rearrange("z (q r) c -> r q z c", r=4)[r].bitcast(I32),
-            )
 
         x_rows = xT.rearrange("(z p j) t -> z j p t", z=PASSES, j=PACK)
         planes = {}
@@ -57,12 +53,17 @@ def tile_picked_relu_e_kernel(
                     nc.sync.dma_start(out=planes[z, j][:], in_=x_rows[z, j])
                 if (z, j) == (0, 0):
                     nc.sync.dma_start(token_list[:], offs)
-                    nc.sync.dma_start(task_list[:], task)
+        nc.sync.dma_start(task_list[:], task)
         nc.sync.dma_start(out=scale_table[:], in_=scale)
         nc.sync.dma_start(
             out=w_codes[:].bitcast(I32),
             in_=w1_words.rearrange("z p c r -> p z (c r)").bitcast(I32),
         )
+        for r in range(4):
+            nc.sync.dma_start(
+                out=w_bytes[r:P:32, :, :].bitcast(I32),
+                in_=w1_scales.rearrange("z (q r) c -> r q z c", r=4)[r].bitcast(I32),
+            )
 
         copy = mybir.ActivationFunctionType.Copy
         list_cols = HALF // LIST_ROWS
@@ -108,23 +109,30 @@ def tile_picked_relu_e_kernel(
         scaled_1 = keep.tile([P, HALF], F32, name="scaled_1")
         gains = (gains_0[:], reused[:, :HALF])
         scaled = (reused[:, HALF:], scaled_1[:])
-        acc = [psum.tile([P, HALF], F32, name=f"acc_{h}") for h in range(HALVES)]
-        for h in range(HALVES):
+        acc = [
+            psum.tile([P, hi - lo], F32, name=f"acc_{i}") for i, (h, lo, hi) in enumerate(OUT_PIECES)
+        ]
+        for half in range(HALVES):
             for z in range(PASSES):
-                nc.tensor.matmul_mx(
-                    out=acc[h][:],
-                    lhsT=w_codes[:, z, :].bitcast(FP8X4),
-                    lhsT_scale=w_bytes[:, z, :],
-                    rhs=x_codes[z, h][:].bitcast(FP8X4),
-                    rhs_scale=x_bytes[z, h][:],
-                    start=(z == 0),
-                    stop=(z == PASSES - 1),
-                )
+                for i, (h, lo, hi) in enumerate(OUT_PIECES):
+                    if h == half:
+                        nc.tensor.matmul_mx(
+                            out=acc[i][:],
+                            lhsT=w_codes[:, z, :].bitcast(FP8X4),
+                            lhsT_scale=w_bytes[:, z, :],
+                            rhs=x_codes[z, h][:, lo:hi].bitcast(FP8X4),
+                            rhs_scale=x_bytes[z, h][:, lo:hi],
+                            start=(z == 0),
+                            stop=(z == PASSES - 1),
+                        )
+        for h in range(HALVES):
             tasks = task_list[:, h * list_cols : (h + 1) * list_cols]
             nc.vector.tensor_copy(gains[h], scale_table[:].indirect(tasks))
-        for h in range(HALVES):
-            nc.vector.tensor_tensor(scaled[h], acc[h][:], gains[h], mybir.AluOpType.mult)
-            result = keep.tile([P, HALF], F32, name=f"result_{h}")
-            nc.scalar.activation(result[:], scaled[h], mybir.ActivationFunctionType.Relu)
-            queue = nc.scalar if h == HALVES - 1 else nc.sync
-            queue.dma_start(out=out[:, h * HALF : (h + 1) * HALF], in_=result[:])
+        for i, (h, lo, hi) in enumerate(OUT_PIECES):
+            nc.vector.tensor_tensor(
+                scaled[h][:, lo:hi], acc[i][:], gains[h][:, lo:hi], mybir.AluOpType.mult
+            )
+            result = keep.tile([P, hi - lo], F32, name=f"result_{i}")
+            nc.scalar.activation(result[:], scaled[h][:, lo:hi], mybir.ActivationFunctionType.Relu)
+            queue = nc.scalar if i == len(OUT_PIECES) - 1 else nc.sync
+            queue.dma_start(out=out[:, h * HALF + lo : h * HALF + hi], in_=result[:])

@@ -73,14 +73,7 @@ def tile_picked_relu_e_kernel(
                 keep.tile([P, HALF, PACK], BF16, name=f"picked_{z}_{h}", align_bytes=64)
                 for h in range(HALVES)
             ]
-            if z == PASSES - 1:
-                dense = keep.tile([P, 2, S], BF16, name="dense")
-                for j in range(2):
-                    nc.vector.tensor_copy(dense[:, j, :], planes[z, j][:].indirect(token_list[:]))
-                for h in range(HALVES):
-                    part = dense[:, :, h * HALF : (h + 1) * HALF]
-                    nc.vector.tensor_copy(picked[h][:, :, 0:2], part.rearrange("p j s -> p s j"))
-            for j in range(2 if z == PASSES - 1 else 0, PACK):
+            for j in range(PACK):
                 plane = planes[z, j]
                 if (z, j) == LAST_PLANE:
                     rounded = keep.tile([P, T], BF16, name="rounded", tag="rounded")

@@ -22,7 +22,7 @@ HALF = S // HALVES
 LIST_ROWS = 16
 LAST_PLANE = (PASSES - 1, PACK - 1)
 LAST_CHUNKS = ((0, 1024), (1024, 1664), (1664, 2048))
-OUT_PIECES = ((0, 0, 256), (1, 0, 128), (1, 128, 256))
+OUT_PIECES = ((0, 0, 128), (0, 128, 256), (1, 0, 128), (1, 128, 256))
 
 
 def tile_picked_relu_e_kernel(
@@ -105,19 +105,17 @@ def tile_picked_relu_e_kernel(
         acc = [
             psum.tile([P, hi - lo], F32, name=f"acc_{i}") for i, (h, lo, hi) in enumerate(OUT_PIECES)
         ]
-        for half in range(HALVES):
+        for i, (h, lo, hi) in enumerate(OUT_PIECES):
             for z in range(PASSES):
-                for i, (h, lo, hi) in enumerate(OUT_PIECES):
-                    if h == half:
-                        nc.tensor.matmul_mx(
-                            out=acc[i][:],
-                            lhsT=w_codes[:, z, :].bitcast(FP8X4),
-                            lhsT_scale=w_bytes[:, z, :],
-                            rhs=x_codes[z, h][:, lo:hi].bitcast(FP8X4),
-                            rhs_scale=x_bytes[z, h][:, lo:hi],
-                            start=(z == 0),
-                            stop=(z == PASSES - 1),
-                        )
+                nc.tensor.matmul_mx(
+                    out=acc[i][:],
+                    lhsT=w_codes[:, z, :].bitcast(FP8X4),
+                    lhsT_scale=w_bytes[:, z, :],
+                    rhs=x_codes[z, h][:, lo:hi].bitcast(FP8X4),
+                    rhs_scale=x_bytes[z, h][:, lo:hi],
+                    start=(z == 0),
+                    stop=(z == PASSES - 1),
+                )
         for h in range(HALVES):
             tasks = task_list[:, h * list_cols : (h + 1) * list_cols]
             nc.vector.tensor_copy(gains[h], scale_table[:].indirect(tasks))
@@ -125,7 +123,11 @@ def tile_picked_relu_e_kernel(
             nc.vector.tensor_tensor(
                 scaled[h][:, lo:hi], acc[i][:], gains[h][:, lo:hi], mybir.AluOpType.mult
             )
-            result = keep.tile([P, hi - lo], F32, name=f"result_{i}")
-            nc.scalar.activation(result[:], scaled[h][:, lo:hi], mybir.ActivationFunctionType.Relu)
-            queue = nc.scalar if i == len(OUT_PIECES) - 1 else nc.sync
-            queue.dma_start(out=out[:, h * HALF + lo : h * HALF + hi], in_=result[:])
+            if lo == 0 or h == 1:
+                result = keep.tile([P, HALF if h == 0 else hi - lo], F32, name=f"result_{i}")
+            part = result[:, lo:hi] if h == 0 else result[:]
+            nc.scalar.activation(part, scaled[h][:, lo:hi], mybir.ActivationFunctionType.Relu)
+            if i > 0:
+                queue = nc.scalar if i == len(OUT_PIECES) - 1 else nc.sync
+                first = 0 if h == 0 else HALF + lo
+                queue.dma_start(out=out[:, first : h * HALF + hi], in_=result[:])

@@ -35,8 +35,8 @@ def tile_picked_relu_e_kernel(
 
         task_list = keep.tile([P, S // LIST_ROWS], U16, name="task_list")
         token_list = keep.tile([P, S // LIST_ROWS], U16, name="token_list")
-        scale_table = keep.tile([P, U], F32, name="scale_table")
-        w_codes = keep.tile([P, PASSES, N], U32, name="w_codes", align_bytes=64)
+        scale_table = keep.tile([P, U], F32, name="scale_table", align_bytes=256)
+        w_codes = keep.tile([P, PASSES, N], U32, name="w_codes", align_bytes=256)
         w_bytes = keep.tile([P, PASSES, N], U8, name="w_bytes", align_bytes=64)
 
         nc.vector.memset(w_bytes[:].rearrange("p z c -> p (z c)").bitcast(I32), 0)
@@ -45,7 +45,7 @@ def tile_picked_relu_e_kernel(
         planes = {}
         for z in range(PASSES):
             for j in range(PACK):
-                planes[z, j] = keep.tile([P, T], F32, name=f"plane_{z}_{j}")
+                planes[z, j] = keep.tile([P, T], F32, name=f"plane_{z}_{j}", align_bytes=256)
                 if (z, j) == LAST_PLANE:
                     for lo, hi in LAST_CHUNKS:
                         nc.sync.dma_start(out=planes[z, j][:, lo:hi], in_=x_rows[z, j][:, lo:hi])
@@ -124,7 +124,7 @@ def tile_picked_relu_e_kernel(
                 scaled[h][:, lo:hi], acc[i][:], gains[h][:, lo:hi], mybir.AluOpType.mult
             )
             if lo == 0 or h == 1:
-                result = keep.tile([P, HALF if h == 0 else hi - lo], F32, name=f"result_{i}")
+                result = keep.tile([P, HALF if h == 0 else hi - lo], F32, name=f"result_{i}", align_bytes=256)
             part = result[:, lo:hi] if h == 0 else result[:]
             nc.scalar.activation(part, scaled[h][:, lo:hi], mybir.ActivationFunctionType.Relu)
             if i > 0:

@@ -128,6 +128,5 @@ def tile_picked_relu_e_kernel(
             part = result[:, lo:hi] if h == 0 else result[:]
             nc.scalar.activation(part, scaled[h][:, lo:hi], mybir.ActivationFunctionType.Relu)
             if i > 0:
-                queue = nc.scalar if i == len(OUT_PIECES) - 1 else nc.sync
                 first = 0 if h == 0 else HALF + lo
-                queue.dma_start(out=out[:, first : h * HALF + hi], in_=result[:])
+                nc.sync.dma_start(out=out[:, first : h * HALF + hi], in_=result[:])

@@ -123,10 +123,8 @@ def tile_picked_relu_e_kernel(
             nc.vector.tensor_tensor(
                 scaled[h][:, lo:hi], acc[i][:], gains[h][:, lo:hi], mybir.AluOpType.mult
             )
-            if lo == 0 or h == 1:
-                result = keep.tile([P, HALF if h == 0 else hi - lo], F32, name=f"result_{i}", align_bytes=256)
-            part = result[:, lo:hi] if h == 0 else result[:]
-            nc.scalar.activation(part, scaled[h][:, lo:hi], mybir.ActivationFunctionType.Relu)
-            if i > 0:
-                first = 0 if h == 0 else HALF + lo
-                nc.sync.dma_start(out=out[:, first : h * HALF + hi], in_=result[:])
+            if lo == 0:
+                result = keep.tile([P, HALF], F32, name=f"result_{h}", align_bytes=256)
+            nc.scalar.activation(result[:, lo:hi], scaled[h][:, lo:hi], mybir.ActivationFunctionType.Relu)
+            if hi == HALF:
+                nc.sync.dma_start(out=out[:, h * HALF : (h + 1) * HALF], in_=result[:])

@@ -23,6 +23,8 @@ LIST_ROWS = 16
 LAST_PLANE = (PASSES - 1, PACK - 1)
 LAST_CHUNKS = ((0, 1024), (1024, 1664), (1664, 2048))
 OUT_PIECES = ((0, 0, 128), (0, 128, 256), (1, 0, 128), (1, 128, 256))
+GROUPS = ((0, 0, 256), (1, 0, 128), (1, 128, 256))
+PIECE = 128
 
 
 def tile_picked_relu_e_kernel(
@@ -102,13 +104,13 @@ def tile_picked_relu_e_kernel(
         scaled_1 = keep.tile([P, HALF], F32, name="scaled_1")
         gains = (gains_0[:], reused[:, :HALF])
         scaled = (reused[:, HALF:], scaled_1[:])
-        acc = [
-            psum.tile([P, hi - lo], F32, name=f"acc_{i}") for i, (h, lo, hi) in enumerate(OUT_PIECES)
-        ]
-        for i, (h, lo, hi) in enumerate(OUT_PIECES):
+        acc = []
+        for i, (h, lo, hi) in enumerate(GROUPS):
+            bank = psum.tile([P, hi - lo], F32, name=f"bank_{i}")
+            acc.extend(bank[:, at : at + PIECE] for at in range(0, hi - lo, PIECE))
             for z in range(PASSES):
                 nc.tensor.matmul_mx(
-                    out=acc[i][:],
+                    out=bank[:],
                     lhsT=w_codes[:, z, :].bitcast(FP8X4),
                     lhsT_scale=w_bytes[:, z, :],
                     rhs=x_codes[z, h][:, lo:hi].bitcast(FP8X4),
@@ -121,7 +123,7 @@ def tile_picked_relu_e_kernel(
             nc.vector.tensor_copy(gains[h], scale_table[:].indirect(tasks))
         for i, (h, lo, hi) in enumerate(OUT_PIECES):
             nc.vector.tensor_tensor(
-                scaled[h][:, lo:hi], acc[i][:], gains[h][:, lo:hi], mybir.AluOpType.mult
+                scaled[h][:, lo:hi], acc[i], gains[h][:, lo:hi], mybir.AluOpType.mult
             )
             if lo == 0:
                 result = keep.tile([P, HALF], F32, name=f"result_{h}", align_bytes=256)

@@ -17,20 +17,18 @@ P = 128
 PACK = 4
 K_PASS = P * PACK
 PASSES = K // K_PASS
-HALVES = 2
-HALF = S // HALVES
 LIST_ROWS = 16
-LAST_PLANE = (PASSES - 1, PACK - 1)
-LAST_CHUNKS = ((0, 1024), (1024, 1664), (1664, 2048))
-OUT_PIECES = ((0, 0, 128), (0, 128, 256), (1, 0, 128), (1, 128, 256))
-GROUPS = ((0, 0, 256), (1, 0, 128), (1, 128, 256))
-PIECE = 128
+HALF = S // 2
+QUARTER = S // 4
+GROUPS = ((0, HALF), (HALF, HALF + QUARTER), (HALF + QUARTER, S))
 
 
 def tile_picked_relu_e_kernel(
     tc, xT, w1_words, w1_scales, scale, offs, task, out
 ):
     nc = tc.nc
+    copy = mybir.ActivationFunctionType.Copy
+    relu = mybir.ActivationFunctionType.Relu
     with ExitStack() as ctx:
         keep = ctx.enter_context(tc.tile_pool(name="keep", bufs=1))
         psum = ctx.enter_context(tc.psum_pool(name="psum", bufs=1))
@@ -40,93 +38,122 @@ def tile_picked_relu_e_kernel(
         scale_table = keep.tile([P, U], F32, name="scale_table", align_bytes=256)
         w_codes = keep.tile([P, PASSES, N], U32, name="w_codes", align_bytes=256)
         w_bytes = keep.tile([P, PASSES, N], U8, name="w_bytes", align_bytes=64)
+        x_0 = keep.tile([P, PACK, T], F32, name="x_0", align_bytes=256)
+        x_1_pair = keep.tile([P, 2, T], F32, name="x_1_pair", align_bytes=256)
+        x_1_third = keep.tile([P, T], F32, name="x_1_third", align_bytes=256)
+        x_1_last = keep.tile([P, T], F32, name="x_1_last", align_bytes=256)
+
+        def tokens(lo, hi):
+            return token_list[:, lo // LIST_ROWS : hi // LIST_ROWS]
+
+        def tasks(lo, hi):
+            return task_list[:, lo // LIST_ROWS : hi // LIST_ROWS]
+
+        def quantise(name, woven, width):
+            codes = keep.tile([P, width], U32, name=f"x_codes_{name}", align_bytes=64)
+            scales = keep.tile([P, width], U8, name=f"x_bytes_{name}", align_bytes=64)
+            nc.vector.quantize_mx(
+                out=codes[:].bitcast(FP8X4),
+                scales=scales[:],
+                in_=woven[:].rearrange("p s j -> p (s j)"),
+            )
+            return codes, scales
 
         nc.vector.memset(w_bytes[:].rearrange("p z c -> p (z c)").bitcast(I32), 0)
 
-        x_rows = xT.rearrange("(z p j) t -> z j p t", z=PASSES, j=PACK)
-        planes = {}
-        for z in range(PASSES):
-            for j in range(PACK):
-                planes[z, j] = keep.tile([P, T], F32, name=f"plane_{z}_{j}", align_bytes=256)
-                if (z, j) == LAST_PLANE:
-                    for lo, hi in LAST_CHUNKS:
-                        nc.sync.dma_start(out=planes[z, j][:, lo:hi], in_=x_rows[z, j][:, lo:hi])
-                else:
-                    nc.sync.dma_start(out=planes[z, j][:], in_=x_rows[z, j])
-                if (z, j) == (0, 0):
-                    nc.sync.dma_start(token_list[:], offs)
+        x_rows = xT.rearrange("(z p j) t -> z p j t", z=PASSES, j=PACK)
+        nc.sync.dma_start(out=x_0[:], in_=x_rows[0])
+        nc.sync.dma_start(token_list[:], offs)
+        nc.sync.dma_start(out=x_1_pair[:], in_=x_rows[1][:, 0:2, :])
+        nc.sync.dma_start(out=x_1_third[:], in_=x_rows[1][:, 2, :])
+        nc.sync.dma_start(out=x_1_last[:], in_=x_rows[1][:, 3, :])
         nc.sync.dma_start(task_list[:], task)
-        nc.sync.dma_start(out=scale_table[:], in_=scale)
-        nc.sync.dma_start(
-            out=w_codes[:].bitcast(I32),
-            in_=w1_words.rearrange("z p c r -> p z (c r)").bitcast(I32),
-        )
         for r in range(4):
             nc.sync.dma_start(
                 out=w_bytes[r:P:32, :, :].bitcast(I32),
                 in_=w1_scales.rearrange("z (q r) c -> r q z c", r=4)[r].bitcast(I32),
             )
+        nc.sync.dma_start(
+            out=w_codes[:].bitcast(I32),
+            in_=w1_words.rearrange("z p c r -> p z (c r)").bitcast(I32),
+        )
+        nc.sync.dma_start(out=scale_table[:], in_=scale)
 
-        copy = mybir.ActivationFunctionType.Copy
-        list_cols = HALF // LIST_ROWS
-        x_codes, x_bytes = {}, {}
+        dense_0 = keep.tile([P, PACK, S], F32, name="dense_0")
+        nc.vector.tensor_copy(dense_0[:, 0, :], x_0[:, 0, :].indirect(token_list[:]))
+        nc.scalar.activation(dense_0[:, 3, :], x_0[:, 3, :].indirect(token_list[:]), copy)
+        nc.vector.tensor_copy(dense_0[:, 1, :], x_0[:, 1, :].indirect(token_list[:]))
+        nc.vector.tensor_copy(dense_0[:, 2, :HALF], x_0[:, 2, :].indirect(tokens(0, HALF)))
+        nc.scalar.activation(dense_0[:, 2, HALF:], x_0[:, 2, :].indirect(tokens(HALF, S)), copy)
+        woven_0 = []
+        for h in range(2):
+            woven_0.append(keep.tile([P, HALF, PACK], BF16, name=f"woven_0_{h}", align_bytes=64))
+            nc.vector.tensor_copy(
+                woven_0[h][:], dense_0[:, :, h * HALF : (h + 1) * HALF].rearrange("p j s -> p s j")
+            )
+        first = [quantise(f"0_{h}", woven_0[h], HALF) for h in range(2)]
+
+        dense_1 = keep.tile([P, PACK - 1, S], F32, name="dense_1")
+        upper = keep.tile([P, 2, QUARTER], F32, name="upper", tag="upper")
+        nc.vector.tensor_copy(dense_1[:, 0, :], x_1_pair[:, 0, :].indirect(token_list[:]))
+        nc.scalar.activation(dense_1[:, 1, :], x_1_pair[:, 1, :].indirect(token_list[:]), copy)
+        b, d, f = (hi for lo, hi in GROUPS)
+        woven_1 = [
+            keep.tile([P, hi - lo, PACK], BF16, name=f"woven_1_{lo}", tag=f"woven_1_{lo}", align_bytes=64)
+            for lo, hi in GROUPS
+        ]
+        nc.vector.tensor_copy(woven_1[2][:, :, 0:2], dense_1[:, 0:2, d:f].rearrange("p j s -> p s j"))
+        nc.vector.tensor_copy(dense_1[:, 2, 0:b], x_1_third[:].indirect(tokens(0, b)))
+        nc.scalar.activation(dense_1[:, 2, b:d], x_1_third[:].indirect(tokens(b, d)), copy)
+        nc.scalar.activation(upper[:, 0, :], x_1_third[:].indirect(tokens(d, f)), copy)
+        nc.vector.tensor_copy(woven_1[1][:, :, 0:3], dense_1[:, :, b:d].rearrange("p j s -> p s j"))
+        nc.vector.tensor_copy(woven_1[0][:, :, 0:3], dense_1[:, :, 0:b].rearrange("p j s -> p s j"))
+
+        last = keep.tile([P, QUARTER], F32, name="last")
+        nc.scalar.activation(last[:], x_1_last[:].indirect(tokens(b, d)), copy)
+        nc.scalar.activation(upper[:, 1, :], x_1_last[:].indirect(tokens(d, f)), copy)
+        nc.vector.tensor_copy(woven_1[0][:, :, 3], x_1_last[:].indirect(tokens(0, b)))
+        nc.vector.tensor_copy(woven_1[1][:, :, 3], last[:])
+        nc.scalar.activation(woven_1[2][:, :, 2:4], upper[:].rearrange("p j s -> p s j"), copy)
+        second = [quantise(f"1_{lo}", woven_1[i], hi - lo) for i, (lo, hi) in enumerate(GROUPS)]
+
+        banks = [psum.tile([P, hi - lo], F32, name=f"bank_{lo}") for lo, hi in GROUPS]
         for z in range(PASSES):
-            picked = [
-                keep.tile([P, HALF, PACK], BF16, name=f"picked_{z}_{h}", align_bytes=64)
-                for h in range(HALVES)
-            ]
-            for j in range(PACK):
-                plane = planes[z, j]
-                if (z, j) == LAST_PLANE:
-                    rounded = keep.tile([P, T], BF16, name="rounded", tag="rounded")
-                    for c, (lo, hi) in enumerate(LAST_CHUNKS):
-                        if c % 2 == 0:
-                            nc.scalar.activation(rounded[:, lo:hi], plane[:, lo:hi], copy)
-                        else:
-                            nc.vector.tensor_copy(rounded[:, lo:hi], plane[:, lo:hi])
-                for h in range(HALVES):
-                    entries = token_list[:, h * list_cols : (h + 1) * list_cols]
-                    if (z, j) == LAST_PLANE and h == HALVES - 1:
-                        nc.scalar.activation(picked[h][:, :, j], rounded[:].indirect(entries), copy)
-                    else:
-                        nc.vector.tensor_copy(picked[h][:, :, j], plane[:].indirect(entries))
-            for h in range(HALVES):
-                x_codes[z, h] = keep.tile([P, HALF], U32, name=f"x_codes_{z}_{h}", align_bytes=64)
-                x_bytes[z, h] = keep.tile([P, HALF], U8, name=f"x_bytes_{z}_{h}", align_bytes=64)
-                nc.vector.quantize_mx(
-                    out=x_codes[z, h][:].bitcast(FP8X4),
-                    scales=x_bytes[z, h][:],
-                    in_=picked[h][:].rearrange("p s j -> p (s j)"),
-                )
-
-        reused = keep.tile([P, 2 * HALF], F32, name="reused", tag="rounded")
-        gains_0 = keep.tile([P, HALF], F32, name="gains_0")
-        scaled_1 = keep.tile([P, HALF], F32, name="scaled_1")
-        gains = (gains_0[:], reused[:, :HALF])
-        scaled = (reused[:, HALF:], scaled_1[:])
-        acc = []
-        for i, (h, lo, hi) in enumerate(GROUPS):
-            bank = psum.tile([P, hi - lo], F32, name=f"bank_{i}")
-            acc.extend(bank[:, at : at + PIECE] for at in range(0, hi - lo, PIECE))
-            for z in range(PASSES):
+            for i, (lo, hi) in enumerate(GROUPS):
+                if z == 0:
+                    codes, scales = first[lo // HALF]
+                    cols = slice(lo % HALF, lo % HALF + hi - lo)
+                else:
+                    codes, scales = second[i]
+                    cols = slice(0, hi - lo)
                 nc.tensor.matmul_mx(
-                    out=bank[:],
+                    out=banks[i][:],
                     lhsT=w_codes[:, z, :].bitcast(FP8X4),
                     lhsT_scale=w_bytes[:, z, :],
-                    rhs=x_codes[z, h][:, lo:hi].bitcast(FP8X4),
-                    rhs_scale=x_bytes[z, h][:, lo:hi],
+                    rhs=codes[:, cols].bitcast(FP8X4),
+                    rhs_scale=scales[:, cols],
                     start=(z == 0),
                     stop=(z == PASSES - 1),
                 )
-        for h in range(HALVES):
-            tasks = task_list[:, h * list_cols : (h + 1) * list_cols]
-            nc.vector.tensor_copy(gains[h], scale_table[:].indirect(tasks))
-        for i, (h, lo, hi) in enumerate(OUT_PIECES):
-            nc.vector.tensor_tensor(
-                scaled[h][:, lo:hi], acc[i], gains[h][:, lo:hi], mybir.AluOpType.mult
-            )
-            if lo == 0:
-                result = keep.tile([P, HALF], F32, name=f"result_{h}", align_bytes=256)
-            nc.scalar.activation(result[:, lo:hi], scaled[h][:, lo:hi], mybir.ActivationFunctionType.Relu)
-            if hi == HALF:
-                nc.sync.dma_start(out=out[:, h * HALF : (h + 1) * HALF], in_=result[:])
+        sums = (banks[0][:, :QUARTER], banks[0][:, QUARTER:], banks[1][:], banks[2][:])
+
+        gains_even = keep.tile([P, 2, QUARTER], F32, name="gains_even", tag=f"woven_1_{d}", align_bytes=64)
+        gains_odd = keep.tile([P, 2, QUARTER], F32, name="gains_odd", tag="upper")
+        gains = (gains_even[:, 0, :], gains_odd[:, 0, :], gains_even[:, 1, :], gains_odd[:, 1, :])
+        for q in range(4):
+            picked = scale_table[:].indirect(tasks(q * QUARTER, (q + 1) * QUARTER))
+            if q % 2 == 0:
+                nc.vector.tensor_copy(gains[q], picked)
+            else:
+                nc.scalar.activation(gains[q], picked, copy)
+        results = [keep.tile([P, HALF], F32, name=f"result_{h}", align_bytes=256) for h in range(2)]
+        for q in range(4):
+            scaled = keep.tile([P, QUARTER], F32, name=f"scaled_{q}")
+            nc.vector.tensor_tensor(scaled[:], sums[q], gains[q], mybir.AluOpType.mult)
+            h, at = divmod(q * QUARTER, HALF)
+            if q == 3:
+                nc.vector.tensor_scalar_max(results[h][:, at : at + QUARTER], scaled[:], 0.0)
+            else:
+                nc.scalar.activation(results[h][:, at : at + QUARTER], scaled[:], relu)
+            if q % 2 == 1:
+                nc.sync.dma_start(out=out[:, h * HALF : (h + 1) * HALF], in_=results[h][:])

@@ -38,8 +38,7 @@ def tile_picked_relu_e_kernel(
         scale_table = keep.tile([P, U], F32, name="scale_table", align_bytes=256)
         w_codes = keep.tile([P, PASSES, N], U32, name="w_codes", align_bytes=256)
         w_bytes = keep.tile([P, PASSES, N], U8, name="w_bytes", align_bytes=64)
-        x_0 = keep.tile([P, PACK, T], F32, name="x_0", align_bytes=256)
-        x_1_pair = keep.tile([P, 2, T], F32, name="x_1_pair", align_bytes=256)
+        x_pairs = [keep.tile([P, 2, T], F32, name=f"x_pair_{u}", align_bytes=256) for u in range(3)]
         x_1_third = keep.tile([P, T], F32, name="x_1_third", align_bytes=256)
         x_1_last = keep.tile([P, T], F32, name="x_1_last", align_bytes=256)
 
@@ -62,9 +61,10 @@ def tile_picked_relu_e_kernel(
         nc.vector.memset(w_bytes[:].rearrange("p z c -> p (z c)").bitcast(I32), 0)
 
         x_rows = xT.rearrange("(z p j) t -> z p j t", z=PASSES, j=PACK)
-        nc.sync.dma_start(out=x_0[:], in_=x_rows[0])
+        nc.sync.dma_start(out=x_pairs[0][:], in_=x_rows[0][:, 0:2, :])
         nc.sync.dma_start(token_list[:], offs)
-        nc.sync.dma_start(out=x_1_pair[:], in_=x_rows[1][:, 0:2, :])
+        nc.sync.dma_start(out=x_pairs[1][:], in_=x_rows[0][:, 2:4, :])
+        nc.sync.dma_start(out=x_pairs[2][:], in_=x_rows[1][:, 0:2, :])
         nc.sync.dma_start(out=x_1_third[:], in_=x_rows[1][:, 2, :])
         nc.sync.dma_start(out=x_1_last[:], in_=x_rows[1][:, 3, :])
         nc.sync.dma_start(task_list[:], task)
@@ -80,11 +80,9 @@ def tile_picked_relu_e_kernel(
         nc.sync.dma_start(out=scale_table[:], in_=scale)
 
         dense_0 = keep.tile([P, PACK, S], F32, name="dense_0")
-        nc.vector.tensor_copy(dense_0[:, 0, :], x_0[:, 0, :].indirect(token_list[:]))
-        nc.scalar.activation(dense_0[:, 3, :], x_0[:, 3, :].indirect(token_list[:]), copy)
-        nc.vector.tensor_copy(dense_0[:, 1, :], x_0[:, 1, :].indirect(token_list[:]))
-        nc.vector.tensor_copy(dense_0[:, 2, :HALF], x_0[:, 2, :].indirect(tokens(0, HALF)))
-        nc.scalar.activation(dense_0[:, 2, HALF:], x_0[:, 2, :].indirect(tokens(HALF, S)), copy)
+        for u in range(2):
+            nc.vector.tensor_copy(dense_0[:, 2 * u, :], x_pairs[u][:, 0, :].indirect(token_list[:]))
+            nc.scalar.activation(dense_0[:, 2 * u + 1, :], x_pairs[u][:, 1, :].indirect(token_list[:]), copy)
         woven_0 = []
         for h in range(2):
             woven_0.append(keep.tile([P, HALF, PACK], BF16, name=f"woven_0_{h}", align_bytes=64))
@@ -93,21 +91,23 @@ def tile_picked_relu_e_kernel(
             )
         first = [quantise(f"0_{h}", woven_0[h], HALF) for h in range(2)]
 
-        dense_1 = keep.tile([P, PACK - 1, S], F32, name="dense_1")
-        upper = keep.tile([P, 2, QUARTER], F32, name="upper", tag="upper")
-        nc.vector.tensor_copy(dense_1[:, 0, :], x_1_pair[:, 0, :].indirect(token_list[:]))
-        nc.scalar.activation(dense_1[:, 1, :], x_1_pair[:, 1, :].indirect(token_list[:]), copy)
+        dense_1 = keep.tile([P, 2, S], F32, name="dense_1")
+        third = keep.tile([P, QUARTER], F32, name="third")
+        upper = keep.tile([P, 2, QUARTER], F32, name="upper")
+        nc.vector.tensor_copy(dense_1[:, 0, :], x_pairs[2][:, 0, :].indirect(token_list[:]))
+        nc.scalar.activation(dense_1[:, 1, :], x_pairs[2][:, 1, :].indirect(token_list[:]), copy)
         b, d, f = (hi for lo, hi in GROUPS)
         woven_1 = [
-            keep.tile([P, hi - lo, PACK], BF16, name=f"woven_1_{lo}", tag=f"woven_1_{lo}", align_bytes=64)
+            keep.tile([P, hi - lo, PACK], BF16, name=f"woven_1_{lo}", align_bytes=64)
             for lo, hi in GROUPS
         ]
-        nc.vector.tensor_copy(woven_1[2][:, :, 0:2], dense_1[:, 0:2, d:f].rearrange("p j s -> p s j"))
-        nc.vector.tensor_copy(dense_1[:, 2, 0:b], x_1_third[:].indirect(tokens(0, b)))
-        nc.scalar.activation(dense_1[:, 2, b:d], x_1_third[:].indirect(tokens(b, d)), copy)
+        nc.vector.tensor_copy(woven_1[0][:, :, 0:2], dense_1[:, :, 0:b].rearrange("p j s -> p s j"))
+        nc.vector.tensor_copy(woven_1[1][:, :, 0:2], dense_1[:, :, b:d].rearrange("p j s -> p s j"))
+        nc.scalar.activation(woven_1[2][:, :, 0:2], dense_1[:, :, d:f].rearrange("p j s -> p s j"), copy)
+        nc.scalar.activation(third[:], x_1_third[:].indirect(tokens(b, d)), copy)
         nc.scalar.activation(upper[:, 0, :], x_1_third[:].indirect(tokens(d, f)), copy)
-        nc.vector.tensor_copy(woven_1[1][:, :, 0:3], dense_1[:, :, b:d].rearrange("p j s -> p s j"))
-        nc.vector.tensor_copy(woven_1[0][:, :, 0:3], dense_1[:, :, 0:b].rearrange("p j s -> p s j"))
+        nc.vector.tensor_copy(woven_1[0][:, :, 2], x_1_third[:].indirect(tokens(0, b)))
+        nc.vector.tensor_copy(woven_1[1][:, :, 2], third[:])
 
         last = keep.tile([P, QUARTER], F32, name="last")
         nc.scalar.activation(last[:], x_1_last[:].indirect(tokens(b, d)), copy)
@@ -137,8 +137,8 @@ def tile_picked_relu_e_kernel(
                 )
         sums = (banks[0][:, :QUARTER], banks[0][:, QUARTER:], banks[1][:], banks[2][:])
 
-        gains_even = keep.tile([P, 2, QUARTER], F32, name="gains_even", tag=f"woven_1_{d}", align_bytes=64)
-        gains_odd = keep.tile([P, 2, QUARTER], F32, name="gains_odd", tag="upper")
+        gains_even = keep.tile([P, 2, QUARTER], F32, name="gains_even")
+        gains_odd = keep.tile([P, 2, QUARTER], F32, name="gains_odd")
         gains = (gains_even[:, 0, :], gains_odd[:, 0, :], gains_even[:, 1, :], gains_odd[:, 1, :])
         for q in range(4):
             picked = scale_table[:].indirect(tasks(q * QUARTER, (q + 1) * QUARTER))

@@ -69,7 +69,7 @@ def tile_picked_relu_e_kernel(
         nc.sync.dma_start(out=x_1_last[:], in_=x_rows[1][:, 3, :])
         nc.sync.dma_start(task_list[:], task)
         for r in range(4):
-            nc.sync.dma_start(
+            nc.scalar.dma_start(
                 out=w_bytes[r:P:32, :, :].bitcast(I32),
                 in_=w1_scales.rearrange("z (q r) c -> r q z c", r=4)[r].bitcast(I32),
             )

@@ -73,11 +73,10 @@ def tile_picked_relu_e_kernel(
                 out=w_bytes[r:P:32, :, :].bitcast(I32),
                 in_=w1_scales.rearrange("z (q r) c -> r q z c", r=4)[r].bitcast(I32),
             )
-        nc.sync.dma_start(
-            out=w_codes[:].bitcast(I32),
-            in_=w1_words.rearrange("z p c r -> p z (c r)").bitcast(I32),
-        )
+        w_rows = w1_words.rearrange("z p c r -> z p (c r)").bitcast(I32)
+        nc.sync.dma_start(out=w_codes[:, 0, :].bitcast(I32), in_=w_rows[0])
         nc.sync.dma_start(out=scale_table[:], in_=scale)
+        nc.sync.dma_start(out=w_codes[:, 1, :].bitcast(I32), in_=w_rows[1])
 
         dense_0 = keep.tile([P, PACK, S], F32, name="dense_0")
         for u in range(2):
@@ -102,54 +101,55 @@ def tile_picked_relu_e_kernel(
             for lo, hi in GROUPS
         ]
         nc.vector.tensor_copy(woven_1[0][:, :, 0:2], dense_1[:, :, 0:b].rearrange("p j s -> p s j"))
-        nc.vector.tensor_copy(woven_1[1][:, :, 0:2], dense_1[:, :, b:d].rearrange("p j s -> p s j"))
-        nc.scalar.activation(woven_1[2][:, :, 0:2], dense_1[:, :, d:f].rearrange("p j s -> p s j"), copy)
-        nc.scalar.activation(third[:], x_1_third[:].indirect(tokens(b, d)), copy)
-        nc.scalar.activation(upper[:, 0, :], x_1_third[:].indirect(tokens(d, f)), copy)
+        nc.vector.tensor_copy(woven_1[2][:, :, 0:2], dense_1[:, :, d:f].rearrange("p j s -> p s j"))
+        nc.scalar.activation(woven_1[1][:, :, 0:2], dense_1[:, :, b:d].rearrange("p j s -> p s j"), copy)
+        nc.scalar.activation(third[:], x_1_third[:].indirect(tokens(d, f)), copy)
+        nc.scalar.activation(upper[:, 0, :], x_1_third[:].indirect(tokens(b, d)), copy)
         nc.vector.tensor_copy(woven_1[0][:, :, 2], x_1_third[:].indirect(tokens(0, b)))
-        nc.vector.tensor_copy(woven_1[1][:, :, 2], third[:])
+        nc.vector.tensor_copy(woven_1[2][:, :, 2], third[:])
 
-        last = keep.tile([P, QUARTER], F32, name="last")
-        nc.scalar.activation(last[:], x_1_last[:].indirect(tokens(b, d)), copy)
-        nc.scalar.activation(upper[:, 1, :], x_1_last[:].indirect(tokens(d, f)), copy)
-        nc.vector.tensor_copy(woven_1[0][:, :, 3], x_1_last[:].indirect(tokens(0, b)))
-        nc.vector.tensor_copy(woven_1[1][:, :, 3], last[:])
-        nc.scalar.activation(woven_1[2][:, :, 2:4], upper[:].rearrange("p j s -> p s j"), copy)
+        last = keep.tile([P, 3, QUARTER], F32, name="last")
+        nc.scalar.activation(upper[:, 1, :], x_1_last[:].indirect(tokens(b, d)), copy)
+        nc.scalar.activation(last[:, 2, :], x_1_last[:].indirect(tokens(d, f)), copy)
+        nc.scalar.activation(woven_1[1][:, :, 2:4], upper[:].rearrange("p j s -> p s j"), copy)
+        for q in range(2):
+            nc.vector.tensor_copy(last[:, q, :], x_1_last[:].indirect(tokens(q * QUARTER, (q + 1) * QUARTER)))
+        for q in range(2):
+            nc.vector.tensor_copy(woven_1[0][:, q * QUARTER : (q + 1) * QUARTER, 3], last[:, q, :])
+        nc.vector.tensor_copy(woven_1[2][:, :, 3], last[:, 2, :])
         second = [quantise(f"1_{lo}", woven_1[i], hi - lo) for i, (lo, hi) in enumerate(GROUPS)]
 
-        banks = [psum.tile([P, hi - lo], F32, name=f"bank_{lo}") for lo, hi in GROUPS]
+        sums = [psum.tile([P, QUARTER], F32, name=f"bank_{q}") for q in range(4)]
         for z in range(PASSES):
-            for i, (lo, hi) in enumerate(GROUPS):
+            for q in range(4):
                 if z == 0:
-                    codes, scales = first[lo // HALF]
-                    cols = slice(lo % HALF, lo % HALF + hi - lo)
+                    codes, scales = first[q // 2]
+                    at = q % 2 * QUARTER
                 else:
-                    codes, scales = second[i]
-                    cols = slice(0, hi - lo)
+                    codes, scales = second[max(q - 1, 0)]
+                    at = QUARTER if q == 1 else 0
                 nc.tensor.matmul_mx(
-                    out=banks[i][:],
+                    out=sums[q][:],
                     lhsT=w_codes[:, z, :].bitcast(FP8X4),
                     lhsT_scale=w_bytes[:, z, :],
-                    rhs=codes[:, cols].bitcast(FP8X4),
-                    rhs_scale=scales[:, cols],
+                    rhs=codes[:, at : at + QUARTER].bitcast(FP8X4),
+                    rhs_scale=scales[:, at : at + QUARTER],
                     start=(z == 0),
                     stop=(z == PASSES - 1),
                 )
-        sums = (banks[0][:, :QUARTER], banks[0][:, QUARTER:], banks[1][:], banks[2][:])
 
-        gains_even = keep.tile([P, 2, QUARTER], F32, name="gains_even")
-        gains_odd = keep.tile([P, 2, QUARTER], F32, name="gains_odd")
-        gains = (gains_even[:, 0, :], gains_odd[:, 0, :], gains_even[:, 1, :], gains_odd[:, 1, :])
+        gains = []
         for q in range(4):
+            gains.append(keep.tile([P, QUARTER], F32, name=f"gains_{q}"))
             picked = scale_table[:].indirect(tasks(q * QUARTER, (q + 1) * QUARTER))
-            if q % 2 == 0:
-                nc.vector.tensor_copy(gains[q], picked)
+            if q == 1:
+                nc.vector.tensor_copy(gains[q][:], picked)
             else:
-                nc.scalar.activation(gains[q], picked, copy)
+                nc.scalar.activation(gains[q][:], picked, copy)
         results = [keep.tile([P, HALF], F32, name=f"result_{h}", align_bytes=256) for h in range(2)]
         for q in range(4):
             scaled = keep.tile([P, QUARTER], F32, name=f"scaled_{q}")
-            nc.vector.tensor_tensor(scaled[:], sums[q], gains[q], mybir.AluOpType.mult)
+            nc.vector.tensor_tensor(scaled[:], sums[q][:], gains[q][:], mybir.AluOpType.mult)
             h, at = divmod(q * QUARTER, HALF)
             if q == 3:
                 nc.vector.tensor_scalar_max(results[h][:, at : at + QUARTER], scaled[:], 0.0)

@@ -38,7 +38,8 @@ def tile_picked_relu_e_kernel(
         scale_table = keep.tile([P, U], F32, name="scale_table", align_bytes=256)
         w_codes = keep.tile([P, PASSES, N], U32, name="w_codes", align_bytes=256)
         w_bytes = keep.tile([P, PASSES, N], U8, name="w_bytes", align_bytes=64)
-        x_pairs = [keep.tile([P, 2, T], F32, name=f"x_pair_{u}", align_bytes=256) for u in range(3)]
+        x_0 = keep.tile([P, PACK, T], F32, name="x_0", align_bytes=256)
+        x_1_pair = keep.tile([P, 2, T], F32, name="x_1_pair", align_bytes=256)
         x_1_third = keep.tile([P, T], F32, name="x_1_third", align_bytes=256)
         x_1_last = keep.tile([P, T], F32, name="x_1_last", align_bytes=256)
 
@@ -54,17 +55,16 @@ def tile_picked_relu_e_kernel(
             nc.vector.quantize_mx(
                 out=codes[:].bitcast(FP8X4),
                 scales=scales[:],
-                in_=woven[:].rearrange("p s j -> p (s j)"),
+                in_=woven.rearrange("p s j -> p (s j)"),
             )
             return codes, scales
 
         nc.vector.memset(w_bytes[:].rearrange("p z c -> p (z c)").bitcast(I32), 0)
 
         x_rows = xT.rearrange("(z p j) t -> z p j t", z=PASSES, j=PACK)
-        nc.sync.dma_start(out=x_pairs[0][:], in_=x_rows[0][:, 0:2, :])
+        nc.sync.dma_start(out=x_0[:], in_=x_rows[0])
         nc.sync.dma_start(token_list[:], offs)
-        nc.sync.dma_start(out=x_pairs[1][:], in_=x_rows[0][:, 2:4, :])
-        nc.sync.dma_start(out=x_pairs[2][:], in_=x_rows[1][:, 0:2, :])
+        nc.sync.dma_start(out=x_1_pair[:], in_=x_rows[1][:, 0:2, :])
         nc.sync.dma_start(out=x_1_third[:], in_=x_rows[1][:, 2, :])
         nc.sync.dma_start(out=x_1_last[:], in_=x_rows[1][:, 3, :])
         nc.sync.dma_start(task_list[:], task)
@@ -79,22 +79,25 @@ def tile_picked_relu_e_kernel(
         nc.sync.dma_start(out=w_codes[:, 1, :].bitcast(I32), in_=w_rows[1])
 
         dense_0 = keep.tile([P, PACK, S], F32, name="dense_0")
-        for u in range(2):
-            nc.vector.tensor_copy(dense_0[:, 2 * u, :], x_pairs[u][:, 0, :].indirect(token_list[:]))
-            nc.scalar.activation(dense_0[:, 2 * u + 1, :], x_pairs[u][:, 1, :].indirect(token_list[:]), copy)
+        for j in range(PACK):
+            nc.vector.tensor_copy(dense_0[:, j, :HALF], x_0[:, j, :].indirect(tokens(0, HALF)))
+        nc.vector.tensor_copy(dense_0[:, 0, HALF:], x_0[:, 0, :].indirect(tokens(HALF, S)))
+        for j in range(1, PACK):
+            nc.scalar.activation(dense_0[:, j, HALF:], x_0[:, j, :].indirect(tokens(HALF, S)), copy)
         woven_0 = []
         for h in range(2):
             woven_0.append(keep.tile([P, HALF, PACK], BF16, name=f"woven_0_{h}", align_bytes=64))
             nc.vector.tensor_copy(
                 woven_0[h][:], dense_0[:, :, h * HALF : (h + 1) * HALF].rearrange("p j s -> p s j")
             )
-        first = [quantise(f"0_{h}", woven_0[h], HALF) for h in range(2)]
+        first = [quantise(f"0_{h}", woven_0[h][:], HALF) for h in range(2)]
 
         dense_1 = keep.tile([P, 2, S], F32, name="dense_1")
         third = keep.tile([P, QUARTER], F32, name="third")
         upper = keep.tile([P, 2, QUARTER], F32, name="upper")
-        nc.vector.tensor_copy(dense_1[:, 0, :], x_pairs[2][:, 0, :].indirect(token_list[:]))
-        nc.scalar.activation(dense_1[:, 1, :], x_pairs[2][:, 1, :].indirect(token_list[:]), copy)
+        nc.vector.tensor_copy(dense_1[:, 0, :HALF], x_1_pair[:, 0, :].indirect(tokens(0, HALF)))
+        nc.scalar.activation(dense_1[:, 1, :], x_1_pair[:, 1, :].indirect(token_list[:]), copy)
+        nc.scalar.activation(dense_1[:, 0, HALF:], x_1_pair[:, 0, :].indirect(tokens(HALF, S)), copy)
         b, d, f = (hi for lo, hi in GROUPS)
         woven_1 = [
             keep.tile([P, hi - lo, PACK], BF16, name=f"woven_1_{lo}", align_bytes=64)
@@ -117,7 +120,8 @@ def tile_picked_relu_e_kernel(
         for q in range(2):
             nc.vector.tensor_copy(woven_1[0][:, q * QUARTER : (q + 1) * QUARTER, 3], last[:, q, :])
         nc.vector.tensor_copy(woven_1[2][:, :, 3], last[:, 2, :])
-        second = [quantise(f"1_{lo}", woven_1[i], hi - lo) for i, (lo, hi) in enumerate(GROUPS)]
+        quarters = (woven_1[0][:, :QUARTER, :], woven_1[0][:, QUARTER:, :], woven_1[1][:], woven_1[2][:])
+        second = [quantise(f"1_{q}", quarters[q], QUARTER) for q in range(4)]
 
         sums = [psum.tile([P, QUARTER], F32, name=f"bank_{q}") for q in range(4)]
         for z in range(PASSES):
@@ -126,8 +130,8 @@ def tile_picked_relu_e_kernel(
                     codes, scales = first[q // 2]
                     at = q % 2 * QUARTER
                 else:
-                    codes, scales = second[max(q - 1, 0)]
-                    at = QUARTER if q == 1 else 0
+                    codes, scales = second[q]
+                    at = 0
                 nc.tensor.matmul_mx(
                     out=sums[q][:],
                     lhsT=w_codes[:, z, :].bitcast(FP8X4),

@@ -20,7 +20,6 @@ PASSES = K // K_PASS
 LIST_ROWS = 16
 HALF = S // 2
 QUARTER = S // 4
-GROUPS = ((0, HALF), (HALF, HALF + QUARTER), (HALF + QUARTER, S))
 
 
 def tile_picked_relu_e_kernel(
@@ -93,34 +92,38 @@ def tile_picked_relu_e_kernel(
         first = [quantise(f"0_{h}", woven_0[h][:], HALF) for h in range(2)]
 
         dense_1 = keep.tile([P, 2, S], F32, name="dense_1")
-        third = keep.tile([P, QUARTER], F32, name="third")
-        upper = keep.tile([P, 2, QUARTER], F32, name="upper")
         nc.vector.tensor_copy(dense_1[:, 0, :HALF], x_1_pair[:, 0, :].indirect(tokens(0, HALF)))
         nc.scalar.activation(dense_1[:, 1, :], x_1_pair[:, 1, :].indirect(token_list[:]), copy)
         nc.scalar.activation(dense_1[:, 0, HALF:], x_1_pair[:, 0, :].indirect(tokens(HALF, S)), copy)
-        b, d, f = (hi for lo, hi in GROUPS)
         woven_1 = [
-            keep.tile([P, hi - lo, PACK], BF16, name=f"woven_1_{lo}", align_bytes=64)
-            for lo, hi in GROUPS
+            keep.tile([P, HALF, PACK], BF16, name=f"woven_1_{h}", align_bytes=64) for h in range(2)
         ]
-        nc.vector.tensor_copy(woven_1[0][:, :, 0:2], dense_1[:, :, 0:b].rearrange("p j s -> p s j"))
-        nc.vector.tensor_copy(woven_1[2][:, :, 0:2], dense_1[:, :, d:f].rearrange("p j s -> p s j"))
-        nc.scalar.activation(woven_1[1][:, :, 0:2], dense_1[:, :, b:d].rearrange("p j s -> p s j"), copy)
-        nc.scalar.activation(third[:], x_1_third[:].indirect(tokens(d, f)), copy)
-        nc.scalar.activation(upper[:, 0, :], x_1_third[:].indirect(tokens(b, d)), copy)
-        nc.vector.tensor_copy(woven_1[0][:, :, 2], x_1_third[:].indirect(tokens(0, b)))
-        nc.vector.tensor_copy(woven_1[2][:, :, 2], third[:])
+        for h in range(2):
+            nc.vector.tensor_copy(
+                woven_1[h][:, :, 0:2], dense_1[:, :, h * HALF : (h + 1) * HALF].rearrange("p j s -> p s j")
+            )
+        quarters = [woven_1[q // 2][:, q % 2 * QUARTER : (q % 2 + 1) * QUARTER, :] for q in range(4)]
 
-        last = keep.tile([P, 3, QUARTER], F32, name="last")
-        nc.scalar.activation(upper[:, 1, :], x_1_last[:].indirect(tokens(b, d)), copy)
-        nc.scalar.activation(last[:, 2, :], x_1_last[:].indirect(tokens(d, f)), copy)
-        nc.scalar.activation(woven_1[1][:, :, 2:4], upper[:].rearrange("p j s -> p s j"), copy)
-        for q in range(2):
+        third = keep.tile([P, 2, QUARTER], F32, name="third")
+        nc.vector.tensor_copy(woven_1[0][:, :, 2], x_1_third[:].indirect(tokens(0, HALF)))
+        for q in (2, 3):
+            nc.scalar.activation(
+                third[:, q - 2, :], x_1_third[:].indirect(tokens(q * QUARTER, (q + 1) * QUARTER)), copy
+            )
+        for q in (2, 3):
+            nc.scalar.activation(quarters[q][:, :, 2], third[:, q - 2, :], copy)
+
+        last = keep.tile([P, 4, QUARTER], F32, name="last")
+        for q in (0, 1):
             nc.vector.tensor_copy(last[:, q, :], x_1_last[:].indirect(tokens(q * QUARTER, (q + 1) * QUARTER)))
-        for q in range(2):
-            nc.vector.tensor_copy(woven_1[0][:, q * QUARTER : (q + 1) * QUARTER, 3], last[:, q, :])
-        nc.vector.tensor_copy(woven_1[2][:, :, 3], last[:, 2, :])
-        quarters = (woven_1[0][:, :QUARTER, :], woven_1[0][:, QUARTER:, :], woven_1[1][:], woven_1[2][:])
+        for q in (2, 3):
+            nc.scalar.activation(
+                last[:, q, :], x_1_last[:].indirect(tokens(q * QUARTER, (q + 1) * QUARTER)), copy
+            )
+        for q in (0, 1):
+            nc.vector.tensor_copy(quarters[q][:, :, 3], last[:, q, :])
+        for q in (2, 3):
+            nc.scalar.activation(quarters[q][:, :, 3], last[:, q, :], copy)
         second = [quantise(f"1_{q}", quarters[q], QUARTER) for q in range(4)]
 
         sums = [psum.tile([P, QUARTER], F32, name=f"bank_{q}") for q in range(4)]
@@ -150,14 +153,15 @@ def tile_picked_relu_e_kernel(
                 nc.vector.tensor_copy(gains[q][:], picked)
             else:
                 nc.scalar.activation(gains[q][:], picked, copy)
-        results = [keep.tile([P, HALF], F32, name=f"result_{h}", align_bytes=256) for h in range(2)]
+        result = keep.tile([P, S], F32, name="result", align_bytes=256)
         for q in range(4):
             scaled = keep.tile([P, QUARTER], F32, name=f"scaled_{q}")
             nc.vector.tensor_tensor(scaled[:], sums[q][:], gains[q][:], mybir.AluOpType.mult)
-            h, at = divmod(q * QUARTER, HALF)
+            lo, hi = q * QUARTER, (q + 1) * QUARTER
             if q == 3:
-                nc.vector.tensor_scalar_max(results[h][:, at : at + QUARTER], scaled[:], 0.0)
+                nc.vector.tensor_scalar_max(result[:, lo:hi], scaled[:], 0.0)
             else:
-                nc.scalar.activation(results[h][:, at : at + QUARTER], scaled[:], relu)
-            if q % 2 == 1:
-                nc.sync.dma_start(out=out[:, h * HALF : (h + 1) * HALF], in_=results[h][:])
+                nc.scalar.activation(result[:, lo:hi], scaled[:], relu)
+            if q != 2:
+                since = min(lo, HALF)
+                nc.sync.dma_start(out=out[:, since:hi], in_=result[:, since:hi])

@@ -87,7 +87,8 @@ def tile_picked_relu_e_kernel(
         for h in range(2):
             woven_0.append(keep.tile([P, HALF, PACK], BF16, name=f"woven_0_{h}", align_bytes=64))
             nc.vector.tensor_copy(
-                woven_0[h][:], dense_0[:, :, h * HALF : (h + 1) * HALF].rearrange("p j s -> p s j")
+                woven_0[h][:].rearrange("p (c i) j -> p c j i", i=4),
+                dense_0[:, :, h * HALF : (h + 1) * HALF].rearrange("p j (c i) -> p c j i", i=4),
             )
         first = [quantise(f"0_{h}", woven_0[h][:], HALF) for h in range(2)]
 
@@ -104,26 +105,18 @@ def tile_picked_relu_e_kernel(
             )
         quarters = [woven_1[q // 2][:, q % 2 * QUARTER : (q % 2 + 1) * QUARTER, :] for q in range(4)]
 
-        third = keep.tile([P, 2, QUARTER], F32, name="third")
-        nc.vector.tensor_copy(woven_1[0][:, :, 2], x_1_third[:].indirect(tokens(0, HALF)))
-        for q in (2, 3):
-            nc.scalar.activation(
-                third[:, q - 2, :], x_1_third[:].indirect(tokens(q * QUARTER, (q + 1) * QUARTER)), copy
-            )
-        for q in (2, 3):
-            nc.scalar.activation(quarters[q][:, :, 2], third[:, q - 2, :], copy)
-
-        last = keep.tile([P, 4, QUARTER], F32, name="last")
-        for q in (0, 1):
-            nc.vector.tensor_copy(last[:, q, :], x_1_last[:].indirect(tokens(q * QUARTER, (q + 1) * QUARTER)))
-        for q in (2, 3):
-            nc.scalar.activation(
-                last[:, q, :], x_1_last[:].indirect(tokens(q * QUARTER, (q + 1) * QUARTER)), copy
-            )
-        for q in (0, 1):
-            nc.vector.tensor_copy(quarters[q][:, :, 3], last[:, q, :])
-        for q in (2, 3):
-            nc.scalar.activation(quarters[q][:, :, 3], last[:, q, :], copy)
+        for j, row in ((2, x_1_third), (3, x_1_last)):
+            dense = keep.tile([P, 4, QUARTER], F32, name=f"dense_1_{j}")
+            for q in (0, 1):
+                nc.vector.tensor_copy(dense[:, q, :], row[:].indirect(tokens(q * QUARTER, (q + 1) * QUARTER)))
+            for q in (2, 3):
+                nc.scalar.activation(
+                    dense[:, q, :], row[:].indirect(tokens(q * QUARTER, (q + 1) * QUARTER)), copy
+                )
+            for q in (0, 1):
+                nc.vector.tensor_copy(quarters[q][:, :, j], dense[:, q, :])
+            for q in (2, 3):
+                nc.scalar.activation(quarters[q][:, :, j], dense[:, q, :], copy)
         second = [quantise(f"1_{q}", quarters[q], QUARTER) for q in range(4)]
 
         sums = [psum.tile([P, QUARTER], F32, name=f"bank_{q}") for q in range(4)]

@@ -20,6 +20,7 @@ PASSES = K // K_PASS
 LIST_ROWS = 16
 HALF = S // 2
 QUARTER = S // 4
+EIGHTH = S // 8
 
 
 def tile_picked_relu_e_kernel(
@@ -115,8 +116,9 @@ def tile_picked_relu_e_kernel(
                 )
             for q in (0, 1):
                 nc.vector.tensor_copy(quarters[q][:, :, j], dense[:, q, :])
-            for q in (2, 3):
-                nc.scalar.activation(quarters[q][:, :, j], dense[:, q, :], copy)
+            nc.scalar.activation(quarters[2][:, :, j], dense[:, 2, :], copy)
+            nc.scalar.activation(quarters[3][:, :EIGHTH, j], dense[:, 3, :EIGHTH], copy)
+            nc.vector.tensor_copy(quarters[3][:, EIGHTH:, j], dense[:, 3, EIGHTH:])
         second = [quantise(f"1_{q}", quarters[q], QUARTER) for q in range(4)]
 
         sums = [psum.tile([P, QUARTER], F32, name=f"bank_{q}") for q in range(4)]
@@ -142,7 +144,7 @@ def tile_picked_relu_e_kernel(
         for q in range(4):
             gains.append(keep.tile([P, QUARTER], F32, name=f"gains_{q}"))
             picked = scale_table[:].indirect(tasks(q * QUARTER, (q + 1) * QUARTER))
-            if q == 1:
+            if q == 2:
                 nc.vector.tensor_copy(gains[q][:], picked)
             else:
                 nc.scalar.activation(gains[q][:], picked, copy)

@@ -59,8 +59,6 @@ def tile_picked_relu_e_kernel(
             )
             return codes, scales
 
-        nc.vector.memset(w_bytes[:].rearrange("p z c -> p (z c)").bitcast(I32), 0)
-
         x_rows = xT.rearrange("(z p j) t -> z p j t", z=PASSES, j=PACK)
         nc.sync.dma_start(out=x_0[:], in_=x_rows[0])
         nc.sync.dma_start(token_list[:], offs)

@@ -151,7 +151,7 @@ def tile_picked_relu_e_kernel(
             scaled = keep.tile([P, QUARTER], F32, name=f"scaled_{q}")
             nc.vector.tensor_tensor(scaled[:], sums[q][:], gains[q][:], mybir.AluOpType.mult)
             lo, hi = q * QUARTER, (q + 1) * QUARTER
-            if q == 3:
+            if q >= 2:
                 nc.vector.tensor_scalar_max(result[:, lo:hi], scaled[:], 0.0)
             else:
                 nc.scalar.activation(result[:, lo:hi], scaled[:], relu)

from contextlib import ExitStack

import concourse.mybir as mybir

K, T, S, N, U = 1024, 2048, 512, 128, 1024
FLOPS = 2 * K * S * N

F32 = mybir.dt.float32
BF16 = mybir.dt.bfloat16
I32 = mybir.dt.int32
U32 = mybir.dt.uint32
U16 = mybir.dt.uint16
U8 = mybir.dt.uint8
FP8X4 = mybir.dt.float8_e4m3fn_x4

P = 128
PACK = 4
K_PASS = P * PACK
PASSES = K // K_PASS
LIST_ROWS = 16
HALF = S // 2
QUARTER = S // 4
EIGHTH = S // 8


def tile_picked_relu_e_kernel(
    tc, xT, w1_words, w1_scales, scale, offs, task, out
):
    nc = tc.nc
    copy = mybir.ActivationFunctionType.Copy
    relu = mybir.ActivationFunctionType.Relu
    with ExitStack() as ctx:
        keep = ctx.enter_context(tc.tile_pool(name="keep", bufs=1))
        psum = ctx.enter_context(tc.psum_pool(name="psum", bufs=1))

        task_list = keep.tile([P, S // LIST_ROWS], U16, name="task_list")
        token_list = keep.tile([P, S // LIST_ROWS], U16, name="token_list")
        scale_table = keep.tile([P, U], F32, name="scale_table", align_bytes=256)
        w_codes = keep.tile([P, PASSES, N], U32, name="w_codes", align_bytes=256)
        w_bytes = keep.tile([P, PASSES, N], U8, name="w_bytes", align_bytes=64)
        x_0 = keep.tile([P, PACK, T], F32, name="x_0", align_bytes=256)
        x_1_pair = keep.tile([P, 2, T], F32, name="x_1_pair", align_bytes=256)
        x_1_third = keep.tile([P, T], F32, name="x_1_third", align_bytes=256)
        x_1_last = keep.tile([P, T], F32, name="x_1_last", align_bytes=256)

        def tokens(lo, hi):
            return token_list[:, lo // LIST_ROWS : hi // LIST_ROWS]

        def tasks(lo, hi):
            return task_list[:, lo // LIST_ROWS : hi // LIST_ROWS]

        def quantise(name, woven, width):
            codes = keep.tile([P, width], U32, name=f"x_codes_{name}", align_bytes=64)
            scales = keep.tile([P, width], U8, name=f"x_bytes_{name}", align_bytes=64)
            nc.vector.quantize_mx(
                out=codes[:].bitcast(FP8X4),
                scales=scales[:],
                in_=woven.rearrange("p s j -> p (s j)"),
            )
            return codes, scales

        x_rows = xT.rearrange("(z p j) t -> z p j t", z=PASSES, j=PACK)
        nc.sync.dma_start(out=x_0[:], in_=x_rows[0])
        nc.sync.dma_start(token_list[:], offs)
        nc.sync.dma_start(out=x_1_pair[:], in_=x_rows[1][:, 0:2, :])
        nc.sync.dma_start(out=x_1_third[:], in_=x_rows[1][:, 2, :])
        nc.sync.dma_start(out=x_1_last[:], in_=x_rows[1][:, 3, :])
        nc.sync.dma_start(task_list[:], task)
        for r in range(4):
            nc.scalar.dma_start(
                out=w_bytes[r:P:32, :, :].bitcast(I32),
                in_=w1_scales.rearrange("z (q r) c -> r q z c", r=4)[r].bitcast(I32),
            )
        w_rows = w1_words.rearrange("z p c r -> z p (c r)").bitcast(I32)
        nc.sync.dma_start(out=w_codes[:, 0, :].bitcast(I32), in_=w_rows[0])
        nc.sync.dma_start(out=scale_table[:], in_=scale)
        nc.sync.dma_start(out=w_codes[:, 1, :].bitcast(I32), in_=w_rows[1])

        dense_0 = keep.tile([P, PACK, S], F32, name="dense_0")
        for j in range(PACK):
            nc.vector.tensor_copy(dense_0[:, j, :HALF], x_0[:, j, :].indirect(tokens(0, HALF)))
        nc.vector.tensor_copy(dense_0[:, 0, HALF:], x_0[:, 0, :].indirect(tokens(HALF, S)))
        for j in range(1, PACK):
            nc.scalar.activation(dense_0[:, j, HALF:], x_0[:, j, :].indirect(tokens(HALF, S)), copy)
        woven_0 = []
        for h in range(2):
            woven_0.append(keep.tile([P, HALF, PACK], BF16, name=f"woven_0_{h}", align_bytes=64))
            nc.vector.tensor_copy(
                woven_0[h][:].rearrange("p (c i) j -> p c j i", i=4),
                dense_0[:, :, h * HALF : (h + 1) * HALF].rearrange("p j (c i) -> p c j i", i=4),
            )
        first = [quantise(f"0_{h}", woven_0[h][:], HALF) for h in range(2)]

        dense_1 = keep.tile([P, 2, S], F32, name="dense_1")
        nc.vector.tensor_copy(dense_1[:, 0, :HALF], x_1_pair[:, 0, :].indirect(tokens(0, HALF)))
        nc.scalar.activation(dense_1[:, 1, :], x_1_pair[:, 1, :].indirect(token_list[:]), copy)
        nc.scalar.activation(dense_1[:, 0, HALF:], x_1_pair[:, 0, :].indirect(tokens(HALF, S)), copy)
        woven_1 = [
            keep.tile([P, HALF, PACK], BF16, name=f"woven_1_{h}", align_bytes=64) for h in range(2)
        ]
        for h in range(2):
            nc.vector.tensor_copy(
                woven_1[h][:, :, 0:2], dense_1[:, :, h * HALF : (h + 1) * HALF].rearrange("p j s -> p s j")
            )
        quarters = [woven_1[q // 2][:, q % 2 * QUARTER : (q % 2 + 1) * QUARTER, :] for q in range(4)]

        for j, row in ((2, x_1_third), (3, x_1_last)):
            dense = keep.tile([P, 4, QUARTER], F32, name=f"dense_1_{j}")
            for q in (0, 1):
                nc.vector.tensor_copy(dense[:, q, :], row[:].indirect(tokens(q * QUARTER, (q + 1) * QUARTER)))
            for q in (2, 3):
                nc.scalar.activation(
                    dense[:, q, :], row[:].indirect(tokens(q * QUARTER, (q + 1) * QUARTER)), copy
                )
            for q in (0, 1):
                nc.vector.tensor_copy(quarters[q][:, :, j], dense[:, q, :])
            nc.scalar.activation(quarters[2][:, :, j], dense[:, 2, :], copy)
            nc.scalar.activation(quarters[3][:, :EIGHTH, j], dense[:, 3, :EIGHTH], copy)
            nc.vector.tensor_copy(quarters[3][:, EIGHTH:, j], dense[:, 3, EIGHTH:])
        second = [quantise(f"1_{q}", quarters[q], QUARTER) for q in range(4)]

        sums = [psum.tile([P, QUARTER], F32, name=f"bank_{q}") for q in range(4)]
        for z in range(PASSES):
            for q in range(4):
                if z == 0:
                    codes, scales = first[q // 2]
                    at = q % 2 * QUARTER
                else:
                    codes, scales = second[q]
                    at = 0
                nc.tensor.matmul_mx(
                    out=sums[q][:],
                    lhsT=w_codes[:, z, :].bitcast(FP8X4),
                    lhsT_scale=w_bytes[:, z, :],
                    rhs=codes[:, at : at + QUARTER].bitcast(FP8X4),
                    rhs_scale=scales[:, at : at + QUARTER],
                    start=(z == 0),
                    stop=(z == PASSES - 1),
                )

        gains = []
        for q in range(4):
            gains.append(keep.tile([P, QUARTER], F32, name=f"gains_{q}"))
            picked = scale_table[:].indirect(tasks(q * QUARTER, (q + 1) * QUARTER))
            if q == 2:
                nc.vector.tensor_copy(gains[q][:], picked)
            else:
                nc.scalar.activation(gains[q][:], picked, copy)
        result = keep.tile([P, S], F32, name="result", align_bytes=256)
        for q in range(4):
            scaled = keep.tile([P, QUARTER], F32, name=f"scaled_{q}")
            nc.vector.tensor_tensor(scaled[:], sums[q][:], gains[q][:], mybir.AluOpType.mult)
            lo, hi = q * QUARTER, (q + 1) * QUARTER
            if q >= 2:
                nc.vector.tensor_scalar_max(result[:, lo:hi], scaled[:], 0.0)
            else:
                nc.scalar.activation(result[:, lo:hi], scaled[:], relu)
            if q != 2:
                since = min(lo, HALF)
                nc.sync.dma_start(out=out[:, since:hi], in_=result[:, since:hi])
